import numpy as np
import ml_dtypes


def mxq(x, axis, fmt="e4m3"):
    dtype, down = {"e4m3": (ml_dtypes.float8_e4m3fn, 7), "e5m2": (ml_dtypes.float8_e5m2, 14)}[fmt]
    v = np.moveaxis(np.asarray(x, np.float32).astype(ml_dtypes.bfloat16).astype(np.float64), axis, -1)
    blocks = v.reshape(v.shape[:-1] + (-1, 32))
    amax = np.abs(blocks).max(-1, keepdims=True)
    byte = np.maximum(np.where(amax > 0, np.frexp(amax)[1] - 1 + 127, 0) - down, 1)
    scale = np.exp2(byte - 127.0)
    codes = (blocks / scale).astype(np.float32).astype(dtype).astype(np.float64)
    return np.moveaxis((codes * scale).reshape(v.shape), -1, axis)


WIDE = False


def mx_kscale(k):
    if not WIDE:
        return np.ones(k)
    levels = np.array([10, -10, 5, -5, 0])
    if k % 512:
        return np.exp2(np.random.permutation(np.resize(levels, k // 32))).repeat(32)
    a = np.empty((k // 512, 16))
    for p in range(k // 512):
        a[p, :8] = np.random.permutation(np.resize(levels, 8))
        for g in range(8):
            far = levels[np.abs(levels - a[p, g]) >= 10]
            a[p, g + 8] = far[np.random.randint(len(far))]
    return np.exp2(a.ravel()).repeat(32)


def f64(x):
    return np.asarray(x).astype(np.float64)


def striped(idx):
    return np.tile(idx.reshape(-1, 16).T, (8, 1)).astype(np.uint16)


def unstriped(offs):
    return offs[:16].T.reshape(-1).astype(np.int64)


def pack_weight(w):
    k, n = w.shape
    w = f64(np.asarray(w, np.float32).astype(ml_dtypes.bfloat16)).reshape(k // 32, 32, n)
    amax = np.abs(w).max(1)
    byte = np.clip(np.where(amax > 0, np.frexp(amax)[1] - 1 + 127 - 7, 1), 1, 254)
    scaled = (w * np.exp2(127.0 - byte)[:, None, :]).reshape(k, n).astype(np.float32)
    words = np.ascontiguousarray(scaled.reshape(k // 512, 128, 4, n).transpose(0, 1, 3, 2)).astype(ml_dtypes.float8_e4m3fn).view(np.uint8)
    return words, np.ascontiguousarray(byte.astype(np.uint8).reshape(k // 512, 16, n))


def unpack_weight(words, scales):
    g, p, n, _ = words.shape
    vals = np.ascontiguousarray(words).view(ml_dtypes.float8_e4m3fn).astype(np.float64) * np.repeat(np.exp2(scales.astype(np.float64) - 127.0), 8, axis=1)[..., None]
    return vals.transpose(0, 1, 3, 2).reshape(g * 512, n)


K, T, E, C, N = 512, 4096, 16, 256, 128


def by_expert(wq, xq):
    return np.concatenate([wq[e].T @ xq[:, e * C:(e + 1) * C] for e in range(E)], axis=1)


def setup_inputs():
    n = np.random.standard_normal
    s = mx_kscale(K)[:, None]
    packed = [pack_weight(m) for m in n((E, K, N)) / np.sqrt(K) / s[None]]
    return {
        "xT": (n((K, T)) * s).astype(np.float32),
        "w_words": np.stack([m[0] for m in packed]),
        "w_scales": np.stack([m[1] for m in packed]),
        "gate": np.tile(np.random.uniform(0.2, 1.0, E * C), (N, 1)).astype(np.float32),
        "offs": striped(np.random.permutation(T)[:E * C]),
    }


def reference(xT, w_words, w_scales, gate, offs):
    idx = unstriped(offs)
    xq = mxq(f64(xT)[:, idx], 0, "e4m3")
    w = np.stack([unpack_weight(w_words[e], w_scales[e]) for e in range(E)])
    y = by_expert(w, xq)
    out = np.zeros((N, T))
    out[:, idx] = f64(gate) * y
    return out

@@ -1,0 +1,163 @@
+from contextlib import ExitStack
+
+import concourse.mybir as mybir
+
+K, T, E, C, N = 512, 4096, 16, 256, 128
+FLOPS = 2 * K * N * E * C
+
+F32 = mybir.dt.float32
+BF16 = mybir.dt.bfloat16
+I32 = mybir.dt.int32
+U32 = mybir.dt.uint32
+U16 = mybir.dt.uint16
+U8 = mybir.dt.uint8
+FP8X4 = mybir.dt.float8_e4m3fn_x4
+MULT = mybir.AluOpType.mult
+
+P = 128
+SLOTS = E * C
+PER_COLUMN = 16
+
+CHUNK = 1024
+CHUNKS = SLOTS // CHUNK
+EXPERTS_PER_CHUNK = CHUNK // C
+EXPERTS_PER_BANK = 2
+
+SPAN = 2048
+
+STAGE = 1024
+LOADS = ((0, 1024), (1024, 1024), (2048, 1024), (3072, 512), (3584, 512))
+VECTOR_CASTS = ((704, 704, 704, 352, 352), (0, 0, 128, 192, 256))
+
+SCATTERS = ((0, 1024), (1024, 1024), (2048, 2048))
+
+
+def tile_routed_moe_kernel(tc, xT, w_words, w_scales, gate, offs, out):
+    nc = tc.nc
+    with ExitStack() as ctx:
+        sbuf = ctx.enter_context(tc.tile_pool(name="sbuf", bufs=1))
+        psum = ctx.enter_context(tc.psum_pool(name="psum", bufs=1))
+
+        offsets = sbuf.tile([P, SLOTS // PER_COLUMN], U16, name="offsets")
+        nc.sync.dma_start(offsets[:], offs)
+
+        rows = xT.rearrange("(p t) m -> p t m", t=4)
+        staged = {}
+        for u in range(2):
+            for s in range(T // STAGE):
+                staged[(u, s)] = sbuf.tile(
+                    [P, 2, STAGE], F32, name="staged%d_%d" % (u, s), tag="bytes%d_%d" % (u, s), align_bytes=64
+                )
+            for first, count in LOADS:
+                at = first % STAGE
+                nc.sync.dma_start(
+                    staged[(u, first // STAGE)][:, :, at : at + count],
+                    rows[:, 2 * u : 2 * u + 2, first : first + count],
+                )
+
+        weight_codes = sbuf.tile([P, E, 4 * N], U8, name="weight_codes", align_bytes=64)
+        nc.sync.dma_start(
+            weight_codes[:].bitcast(I32), w_words.rearrange("e a p n r -> p (e a) (n r)").bitcast(I32)
+        )
+        weight_scales = sbuf.tile([P, E * N], U8, name="weight_scales", align_bytes=64)
+        nc.vector.memset(weight_scales[:].bitcast(I32), 0)
+        for quadrant in range(4):
+            nc.sync.dma_start(
+                weight_scales[32 * quadrant : 32 * quadrant + 4, :].bitcast(I32).rearrange("q (e n) -> q e n", e=E),
+                w_scales[:, 0, 4 * quadrant : 4 * quadrant + 4, :].bitcast(I32).rearrange("e q n -> q e n"),
+            )
+        gates = sbuf.tile([P, SLOTS], F32, name="gates")
+        for c in range(CHUNKS):
+            nc.sync.dma_start(gates[:, c * CHUNK : (c + 1) * CHUNK], gate[:, c * CHUNK : (c + 1) * CHUNK])
+
+        window = [sbuf.tile([P, T, 2], BF16, name="window%d" % u) for u in range(2)]
+        picked = [sbuf.tile([P, 2, SPAN], U32, name="picked%d" % h) for h in range(SLOTS // SPAN)]
+        grouped = [
+            sbuf.tile([P, 4 * CHUNK], BF16, name="grouped%d" % c, tag="bytes1_%d" % c, align_bytes=64)
+            for c in range(CHUNKS)
+        ]
+        slot_codes = [sbuf.tile([P, CHUNK], U32, name="slot_codes%d" % c, align_bytes=64) for c in range(CHUNKS)]
+        slot_scales = [sbuf.tile([P, CHUNK], U8, name="slot_scales%d" % c, align_bytes=64) for c in range(CHUNKS)]
+        sums = sbuf.tile([P, SLOTS], F32, name="sums")
+        result = sbuf.tile([P, T], F32, name="result")
+
+        def cast(copy, u, first, count):
+            at = first % STAGE
+            copy(
+                out=window[u][:, first : first + count, :],
+                in_=staged[(u, first // STAGE)][:, :, at : at + count].rearrange("p i m -> p m i"),
+            )
+
+        def listed(first, count):
+            return offsets[:, first // PER_COLUMN : (first + count) // PER_COLUMN]
+
+        def gather(u, first, count):
+            at = first % SPAN
+            nc.vector.tensor_copy(
+                out=picked[first // SPAN][:, u, at : at + count],
+                in_=window[u][:].rearrange("p m i -> p (m i)").bitcast(U32).indirect(listed(first, count)),
+            )
+
+        def interleave(c):
+            at = c * CHUNK % SPAN
+            nc.scalar.copy(
+                out=grouped[c][:].bitcast(U32).rearrange("p (d u) -> p d u", u=2),
+                in_=picked[c * CHUNK // SPAN][:, :, at : at + CHUNK].rearrange("p u d -> p d u"),
+            )
+
+        def quantise(c):
+            nc.vector.quantize_mx(out=slot_codes[c][:].bitcast(FP8X4), scales=slot_scales[c][:], in_=grouped[c][:])
+
+        def multiply(c):
+            for bank_no in range(EXPERTS_PER_CHUNK // EXPERTS_PER_BANK):
+                bank = psum.tile([P, EXPERTS_PER_BANK * C], F32, name="bank%d_%d" % (c, bank_no))
+                for side in range(EXPERTS_PER_BANK):
+                    at = (bank_no * EXPERTS_PER_BANK + side) * C
+                    e = (c * CHUNK + at) // C
+                    nc.tensor.matmul_mx(
+                        out=bank[:, side * C : (side + 1) * C],
+                        lhsT=weight_codes[:, e, :].bitcast(FP8X4),
+                        lhsT_scale=weight_scales[:, e * N : (e + 1) * N],
+                        rhs=slot_codes[c][:, at : at + C].bitcast(FP8X4),
+                        rhs_scale=slot_scales[c][:, at : at + C],
+                        start=True,
+                        stop=True,
+                    )
+                first = c * CHUNK + bank_no * EXPERTS_PER_BANK * C
+                nc.scalar.copy(out=sums[:, first : first + EXPERTS_PER_BANK * C], in_=bank[:])
+
+        def scatter(first, count):
+            nc.vector.tensor_tensor(
+                out=result[:].indirect(listed(first, count)),
+                in0=sums[:, first : first + count],
+                in1=gates[:, first : first + count],
+                op=MULT,
+            )
+
+        for (first, count), by_vector in zip(LOADS, VECTOR_CASTS[0]):
+            cast(nc.vector.tensor_copy, 0, first, by_vector)
+            cast(nc.scalar.copy, 0, first + by_vector, count - by_vector)
+        for (first, count), by_vector in zip(LOADS, VECTOR_CASTS[1]):
+            cast(nc.scalar.copy, 1, first + by_vector, count - by_vector)
+
+        for first in range(0, SLOTS, SPAN):
+            gather(0, first, SPAN)
+        for (first, count), by_vector in zip(LOADS, VECTOR_CASTS[1]):
+            if by_vector:
+                cast(nc.vector.tensor_copy, 1, first, by_vector)
+
+        for c in range(CHUNKS):
+            gather(1, c * CHUNK, CHUNK)
+            interleave(c)
+            if c > 0:
+                quantise(c - 1)
+                multiply(c - 1)
+        scatter(*SCATTERS[0])
+        quantise(CHUNKS - 1)
+        multiply(CHUNKS - 1)
+        for first, count in SCATTERS[1:]:
+            scatter(first, count)
+
+        quarter = T // 4
+        for h, queue in enumerate((nc.sync, nc.scalar, nc.sync, nc.scalar)):
+            queue.dma_start(out[:, h * quarter : (h + 1) * quarter], result[:, h * quarter : (h + 1) * quarter])

@@ -26,8 +26,8 @@ EXPERTS_PER_BANK = 2
 SPAN = 2048
 
 STAGE = 1024
-LOADS = ((0, 1024), (1024, 1024), (2048, 1024), (3072, 512), (3584, 512))
-VECTOR_CASTS = ((704, 704, 704, 352, 352), (0, 0, 128, 192, 256))
+LOADS = (((0, 1024), (1024, 1024), (2048, 1024), (3072, 512), (3584, 512)), ((0, 256), (256, 768), (1024, 1024), (2048, 1024), (3072, 512), (3584, 512)))
+VECTOR_CASTS = ((704, 704, 704, 352, 352), (0, 0, 0, 0, 128, 320))
 
 SCATTERS = ((0, 1024), (1024, 1024), (2048, 2048))
 
@@ -48,7 +48,7 @@ def tile_routed_moe_kernel(tc, xT, w_words, w_scales, gate, offs, out):
                 staged[(u, s)] = sbuf.tile(
                     [P, 2, STAGE], F32, name="staged%d_%d" % (u, s), tag="bytes%d_%d" % (u, s), align_bytes=64
                 )
-            for first, count in LOADS:
+            for first, count in LOADS[u]:
                 at = first % STAGE
                 nc.sync.dma_start(
                     staged[(u, first // STAGE)][:, :, at : at + count],
@@ -134,28 +134,26 @@ def tile_routed_moe_kernel(tc, xT, w_words, w_scales, gate, offs, out):
                 op=MULT,
             )
 
-        for (first, count), by_vector in zip(LOADS, VECTOR_CASTS[0]):
+        for (first, count), by_vector in zip(LOADS[0], VECTOR_CASTS[0]):
             cast(nc.vector.tensor_copy, 0, first, by_vector)
             cast(nc.scalar.copy, 0, first + by_vector, count - by_vector)
-        for (first, count), by_vector in zip(LOADS, VECTOR_CASTS[1]):
-            cast(nc.scalar.copy, 1, first + by_vector, count - by_vector)
+        for (first, count), by_vector in zip(LOADS[1], VECTOR_CASTS[1]):
+            if count > by_vector:
+                cast(nc.scalar.copy, 1, first + by_vector, count - by_vector)
 
         for first in range(0, SLOTS, SPAN):
             gather(0, first, SPAN)
-        for (first, count), by_vector in zip(LOADS, VECTOR_CASTS[1]):
+        for (first, count), by_vector in zip(LOADS[1], VECTOR_CASTS[1]):
             if by_vector:
                 cast(nc.vector.tensor_copy, 1, first, by_vector)
 
         for c in range(CHUNKS):
             gather(1, c * CHUNK, CHUNK)
             interleave(c)
-            if c > 0:
-                quantise(c - 1)
-                multiply(c - 1)
-        scatter(*SCATTERS[0])
-        quantise(CHUNKS - 1)
-        multiply(CHUNKS - 1)
-        for first, count in SCATTERS[1:]:
+        for c in range(CHUNKS):
+            quantise(c)
+            multiply(c)
+        for first, count in SCATTERS:
             scatter(first, count)
 
         quarter = T // 4

@@ -26,10 +26,10 @@ EXPERTS_PER_BANK = 2
 SPAN = 2048
 
 STAGE = 1024
-LOADS = (((0, 1024), (1024, 1024), (2048, 1024), (3072, 512), (3584, 512)), ((0, 256), (256, 768), (1024, 1024), (2048, 1024), (3072, 512), (3584, 512)))
-VECTOR_CASTS = ((704, 704, 704, 352, 352), (0, 0, 0, 0, 128, 320))
+LOADS = (((0, 1024), (1024, 1024), (2048, 1024), (3072, 512), (3584, 256), (3840, 256)), ((0, 256), (256, 768), (1024, 1024), (2048, 1024), (3072, 512), (3584, 512)))
+VECTOR_CASTS = ((704, 704, 704, 352, 176, 256), (0, 0, 0, 0, 128, 320))
 
-SCATTERS = ((0, 1024), (1024, 1024), (2048, 2048))
+SCATTERS = ((0, 2048), (2048, 2048))
 
 
 def tile_routed_moe_kernel(tc, xT, w_words, w_scales, gate, offs, out):
@@ -39,7 +39,6 @@ def tile_routed_moe_kernel(tc, xT, w_words, w_scales, gate, offs, out):
         psum = ctx.enter_context(tc.psum_pool(name="psum", bufs=1))
 
         offsets = sbuf.tile([P, SLOTS // PER_COLUMN], U16, name="offsets")
-        nc.sync.dma_start(offsets[:], offs)
 
         rows = xT.rearrange("(p t) m -> p t m", t=4)
         staged = {}
@@ -54,6 +53,8 @@ def tile_routed_moe_kernel(tc, xT, w_words, w_scales, gate, offs, out):
                     staged[(u, first // STAGE)][:, :, at : at + count],
                     rows[:, 2 * u : 2 * u + 2, first : first + count],
                 )
+            if u == 0:
+                nc.sync.dma_start(offsets[:], offs)
 
         weight_codes = sbuf.tile([P, E, 4 * N], U8, name="weight_codes", align_bytes=64)
         nc.sync.dma_start(
@@ -67,8 +68,8 @@ def tile_routed_moe_kernel(tc, xT, w_words, w_scales, gate, offs, out):
                 w_scales[:, 0, 4 * quadrant : 4 * quadrant + 4, :].bitcast(I32).rearrange("e q n -> q e n"),
             )
         gates = sbuf.tile([P, SLOTS], F32, name="gates")
-        for c in range(CHUNKS):
-            nc.sync.dma_start(gates[:, c * CHUNK : (c + 1) * CHUNK], gate[:, c * CHUNK : (c + 1) * CHUNK])
+        for first, count in SCATTERS:
+            nc.sync.dma_start(gates[:, first : first + count], gate[:, first : first + count])
 
         window = [sbuf.tile([P, T, 2], BF16, name="window%d" % u) for u in range(2)]
         picked = [sbuf.tile([P, 2, SPAN], U32, name="picked%d" % h) for h in range(SLOTS // SPAN)]
@@ -136,7 +137,8 @@ def tile_routed_moe_kernel(tc, xT, w_words, w_scales, gate, offs, out):
 
         for (first, count), by_vector in zip(LOADS[0], VECTOR_CASTS[0]):
             cast(nc.vector.tensor_copy, 0, first, by_vector)
-            cast(nc.scalar.copy, 0, first + by_vector, count - by_vector)
+            if count > by_vector:
+                cast(nc.scalar.copy, 0, first + by_vector, count - by_vector)
         for (first, count), by_vector in zip(LOADS[1], VECTOR_CASTS[1]):
             if count > by_vector:
                 cast(nc.scalar.copy, 1, first + by_vector, count - by_vector)

@@ -26,8 +26,9 @@ EXPERTS_PER_BANK = 2
 SPAN = 2048
 
 STAGE = 1024
-LOADS = (((0, 1024), (1024, 1024), (2048, 1024), (3072, 512), (3584, 256), (3840, 256)), ((0, 256), (256, 768), (1024, 1024), (2048, 1024), (3072, 512), (3584, 512)))
-VECTOR_CASTS = ((704, 704, 704, 352, 176, 256), (0, 0, 0, 0, 128, 320))
+LOADS = (((0, 1024), (1024, 1024), (2048, 1024), (3072, 512), (3584, 256), (3840, 256)), ((0, 256), (256, 768), (1024, 1024), (2048, 1024), (3072, 512), (3584, 256), (3840, 256)))
+VECTOR_CASTS = ((704, 704, 704, 352, 176, 256), (0, 0, 0, 0, 0, 0, 256))
+GPSIMD_CASTS = (0, 256, 384, 384, 0, 0, 0)
 
 SCATTERS = ((0, 2048), (2048, 2048))
 
@@ -139,9 +140,14 @@ def tile_routed_moe_kernel(tc, xT, w_words, w_scales, gate, offs, out):
             cast(nc.vector.tensor_copy, 0, first, by_vector)
             if count > by_vector:
                 cast(nc.scalar.copy, 0, first + by_vector, count - by_vector)
-        for (first, count), by_vector in zip(LOADS[1], VECTOR_CASTS[1]):
-            if count > by_vector:
-                cast(nc.scalar.copy, 1, first + by_vector, count - by_vector)
+        def gpsimd_copy(out, in_):
+            nc.gpsimd.tensor_scalar(out=out, in0=in_, scalar1=1.0, scalar2=0.0, op0=MULT, op1=mybir.AluOpType.add)
+
+        for (first, count), by_gpsimd, by_vector in zip(LOADS[1], GPSIMD_CASTS, VECTOR_CASTS[1]):
+            if count > by_gpsimd + by_vector:
+                cast(nc.scalar.copy, 1, first + by_vector, count - by_gpsimd - by_vector)
+            if by_gpsimd:
+                cast(gpsimd_copy, 1, first + count - by_gpsimd, by_gpsimd)
 
         for first in range(0, SLOTS, SPAN):
             gather(0, first, SPAN)

@@ -27,8 +27,8 @@ SPAN = 2048
 
 STAGE = 1024
 LOADS = (((0, 1024), (1024, 1024), (2048, 1024), (3072, 512), (3584, 256), (3840, 256)), ((0, 256), (256, 768), (1024, 1024), (2048, 1024), (3072, 512), (3584, 256), (3840, 256)))
-VECTOR_CASTS = ((704, 704, 704, 352, 176, 256), (0, 0, 0, 0, 0, 0, 256))
-GPSIMD_CASTS = (0, 256, 384, 384, 0, 0, 0)
+VECTOR_CASTS = ((704, 704, 704, 352, 176, 256), (0, 0, 0, 0, 0, 0, 0))
+GPSIMD_CASTS = (0, 256, 384, 384, 0, 0, 128)
 
 SCATTERS = ((0, 2048), (2048, 2048))
 

@@ -26,9 +26,9 @@ EXPERTS_PER_BANK = 2
 SPAN = 2048
 
 STAGE = 1024
-LOADS = (((0, 1024), (1024, 1024), (2048, 1024), (3072, 512), (3584, 256), (3840, 256)), ((0, 256), (256, 768), (1024, 1024), (2048, 1024), (3072, 512), (3584, 256), (3840, 256)))
-VECTOR_CASTS = ((704, 704, 704, 352, 176, 256), (0, 0, 0, 0, 0, 0, 0))
-GPSIMD_CASTS = (0, 256, 384, 384, 0, 0, 128)
+LOADS = (((0, 1024), (1024, 1024), (2048, 1024), (3072, 512), (3584, 384), (3968, 128)), ((0, 256), (256, 768), (1024, 1024), (2048, 1024), (3072, 512), (3584, 384), (3968, 128)))
+VECTOR_CASTS = ((704, 704, 704, 352, 272, 0), (0, 0, 0, 0, 0, 0, 0))
+GPSIMD_CASTS = (0, 256, 384, 512, 224, 224, 0)
 
 SCATTERS = ((0, 2048), (2048, 2048))
 
@@ -137,7 +137,8 @@ def tile_routed_moe_kernel(tc, xT, w_words, w_scales, gate, offs, out):
             )
 
         for (first, count), by_vector in zip(LOADS[0], VECTOR_CASTS[0]):
-            cast(nc.vector.tensor_copy, 0, first, by_vector)
+            if by_vector:
+                cast(nc.vector.tensor_copy, 0, first, by_vector)
             if count > by_vector:
                 cast(nc.scalar.copy, 0, first + by_vector, count - by_vector)
         def gpsimd_copy(out, in_):

@@ -28,7 +28,7 @@ SPAN = 2048
 STAGE = 1024
 LOADS = (((0, 1024), (1024, 1024), (2048, 1024), (3072, 512), (3584, 384), (3968, 128)), ((0, 256), (256, 768), (1024, 1024), (2048, 1024), (3072, 512), (3584, 384), (3968, 128)))
 VECTOR_CASTS = ((704, 704, 704, 352, 272, 0), (0, 0, 0, 0, 0, 0, 0))
-GPSIMD_CASTS = (0, 256, 384, 512, 224, 224, 0)
+GPSIMD_CASTS = (0, 0, 128, 512, 224, 224, 0)
 
 SCATTERS = ((0, 2048), (2048, 2048))
 

@@ -54,8 +54,8 @@ def tile_routed_moe_kernel(tc, xT, w_words, w_scales, gate, offs, out):
                     staged[(u, first // STAGE)][:, :, at : at + count],
                     rows[:, 2 * u : 2 * u + 2, first : first + count],
                 )
-            if u == 0:
-                nc.sync.dma_start(offsets[:], offs)
+                if u == 0 and first == 0:
+                    nc.sync.dma_start(offsets[:], offs)
 
         weight_codes = sbuf.tile([P, E, 4 * N], U8, name="weight_codes", align_bytes=64)
         nc.sync.dma_start(

@@ -25,10 +25,10 @@ EXPERTS_PER_BANK = 2
 
 SPAN = 2048
 
-STAGE = 1024
-LOADS = (((0, 1024), (1024, 1024), (2048, 1024), (3072, 512), (3584, 384), (3968, 128)), ((0, 256), (256, 768), (1024, 1024), (2048, 1024), (3072, 512), (3584, 384), (3968, 128)))
-VECTOR_CASTS = ((704, 704, 704, 352, 272, 0), (0, 0, 0, 0, 0, 0, 0))
-GPSIMD_CASTS = (0, 0, 128, 512, 224, 224, 0)
+STAGE = (1024, 2048)
+LOADS = (((0, 1024), (1024, 1024), (2048, 1024), (3072, 512), (3584, 384), (3968, 128)), ((0, 256), (256, 1792), (2048, 1024), (3072, 512), (3584, 384), (3968, 128)))
+VECTOR_CASTS = ((704, 704, 704, 352, 272, 0), (0, 0, 0, 0, 0, 0))
+GPSIMD_CASTS = (0, 832, 448, 224, 224, 0)
 
 SCATTERS = ((0, 2048), (2048, 2048))
 
@@ -44,14 +44,14 @@ def tile_routed_moe_kernel(tc, xT, w_words, w_scales, gate, offs, out):
         rows = xT.rearrange("(p t) m -> p t m", t=4)
         staged = {}
         for u in range(2):
-            for s in range(T // STAGE):
+            for s in range(T // STAGE[u]):
                 staged[(u, s)] = sbuf.tile(
-                    [P, 2, STAGE], F32, name="staged%d_%d" % (u, s), tag="bytes%d_%d" % (u, s), align_bytes=64
+                    [P, 2, STAGE[u]], F32, name="staged%d_%d" % (u, s), tag="bytes%d_%d" % (u, s), align_bytes=64
                 )
             for first, count in LOADS[u]:
-                at = first % STAGE
+                at = first % STAGE[u]
                 nc.sync.dma_start(
-                    staged[(u, first // STAGE)][:, :, at : at + count],
+                    staged[(u, first // STAGE[u])][:, :, at : at + count],
                     rows[:, 2 * u : 2 * u + 2, first : first + count],
                 )
                 if u == 0 and first == 0:
@@ -75,8 +75,8 @@ def tile_routed_moe_kernel(tc, xT, w_words, w_scales, gate, offs, out):
         window = [sbuf.tile([P, T, 2], BF16, name="window%d" % u) for u in range(2)]
         picked = [sbuf.tile([P, 2, SPAN], U32, name="picked%d" % h) for h in range(SLOTS // SPAN)]
         grouped = [
-            sbuf.tile([P, 4 * CHUNK], BF16, name="grouped%d" % c, tag="bytes1_%d" % c, align_bytes=64)
-            for c in range(CHUNKS)
+            sbuf.tile([P, 4 * SPAN], BF16, name="grouped%d" % h, tag="bytes1_%d" % h, align_bytes=64)
+            for h in range(SLOTS // SPAN)
         ]
         slot_codes = [sbuf.tile([P, CHUNK], U32, name="slot_codes%d" % c, align_bytes=64) for c in range(CHUNKS)]
         slot_scales = [sbuf.tile([P, CHUNK], U8, name="slot_scales%d" % c, align_bytes=64) for c in range(CHUNKS)]
@@ -84,10 +84,10 @@ def tile_routed_moe_kernel(tc, xT, w_words, w_scales, gate, offs, out):
         result = sbuf.tile([P, T], F32, name="result")
 
         def cast(copy, u, first, count):
-            at = first % STAGE
+            at = first % STAGE[u]
             copy(
                 out=window[u][:, first : first + count, :],
-                in_=staged[(u, first // STAGE)][:, :, at : at + count].rearrange("p i m -> p m i"),
+                in_=staged[(u, first // STAGE[u])][:, :, at : at + count].rearrange("p i m -> p m i"),
             )
 
         def listed(first, count):
@@ -100,15 +100,19 @@ def tile_routed_moe_kernel(tc, xT, w_words, w_scales, gate, offs, out):
                 in_=window[u][:].rearrange("p m i -> p (m i)").bitcast(U32).indirect(listed(first, count)),
             )
 
+        def four_values(c):
+            at = c * CHUNK % SPAN
+            return grouped[c * CHUNK // SPAN][:, 4 * at : 4 * (at + CHUNK)]
+
         def interleave(c):
             at = c * CHUNK % SPAN
             nc.scalar.copy(
-                out=grouped[c][:].bitcast(U32).rearrange("p (d u) -> p d u", u=2),
+                out=four_values(c).bitcast(U32).rearrange("p (d u) -> p d u", u=2),
                 in_=picked[c * CHUNK // SPAN][:, :, at : at + CHUNK].rearrange("p u d -> p d u"),
             )
 
         def quantise(c):
-            nc.vector.quantize_mx(out=slot_codes[c][:].bitcast(FP8X4), scales=slot_scales[c][:], in_=grouped[c][:])
+            nc.vector.quantize_mx(out=slot_codes[c][:].bitcast(FP8X4), scales=slot_scales[c][:], in_=four_values(c))
 
         def multiply(c):
             for bank_no in range(EXPERTS_PER_CHUNK // EXPERTS_PER_BANK):

@@ -25,10 +25,25 @@ EXPERTS_PER_BANK = 2
 
 SPAN = 2048
 
-STAGE = (1024, 2048)
-LOADS = (((0, 1024), (1024, 1024), (2048, 1024), (3072, 512), (3584, 384), (3968, 128)), ((0, 256), (256, 1792), (2048, 1024), (3072, 512), (3584, 384), (3968, 128)))
-VECTOR_CASTS = ((704, 704, 704, 352, 272, 0), (0, 0, 0, 0, 0, 0))
-GPSIMD_CASTS = (0, 832, 448, 224, 224, 0)
+EARLY = 3072
+
+STAGE = (4096, 2048)
+LOADS = (
+    ((0, 2, 0, 1792), (0, 1, 1792, 2304), (1, 2, 1792, 1024), (1, 2, 2816, 1280)),
+    ((0, 2, 0, 256), (0, 2, 256, 768), (0, 2, 1024, 1024), (0, 2, 2048, 1024), (0, 2, 3072, 512), (0, 2, 3584, 256), (0, 2, 3840, 256)),
+)
+CASTS = (
+    (0, 0, 1152, 640, 0),
+    (0, 1792, 0, 576, 448),
+    (0, 2816, 0, 704, 576),
+    (1, 0, 0, 256, 0),
+    (1, 256, 0, 0, 768),
+    (1, 1024, 0, 576, 448),
+    (1, 2048, 0, 576, 448),
+    (1, 3072, 0, 288, 224),
+    (1, 3584, 0, 144, 112),
+    (1, 3840, 0, 144, 112),
+)
 
 SCATTERS = ((0, 2048), (2048, 2048))
 
@@ -48,11 +63,11 @@ def tile_routed_moe_kernel(tc, xT, w_words, w_scales, gate, offs, out):
                 staged[(u, s)] = sbuf.tile(
                     [P, 2, STAGE[u]], F32, name="staged%d_%d" % (u, s), tag="bytes%d_%d" % (u, s), align_bytes=64
                 )
-            for first, count in LOADS[u]:
+            for row, end, first, count in LOADS[u]:
                 at = first % STAGE[u]
                 nc.sync.dma_start(
-                    staged[(u, first // STAGE[u])][:, :, at : at + count],
-                    rows[:, 2 * u : 2 * u + 2, first : first + count],
+                    staged[(u, first // STAGE[u])][:, row:end, at : at + count],
+                    rows[:, 2 * u + row : 2 * u + end, first : first + count],
                 )
                 if u == 0 and first == 0:
                     nc.sync.dma_start(offsets[:], offs)
@@ -74,6 +89,7 @@ def tile_routed_moe_kernel(tc, xT, w_words, w_scales, gate, offs, out):
 
         window = [sbuf.tile([P, T, 2], BF16, name="window%d" % u) for u in range(2)]
         picked = [sbuf.tile([P, 2, SPAN], U32, name="picked%d" % h) for h in range(SLOTS // SPAN)]
+        early = sbuf.tile([P, 2, SLOTS - EARLY], F32, name="early")
         grouped = [
             sbuf.tile([P, 4 * SPAN], BF16, name="grouped%d" % h, tag="bytes1_%d" % h, align_bytes=64)
             for h in range(SLOTS // SPAN)
@@ -140,25 +156,23 @@ def tile_routed_moe_kernel(tc, xT, w_words, w_scales, gate, offs, out):
                 op=MULT,
             )
 
-        for (first, count), by_vector in zip(LOADS[0], VECTOR_CASTS[0]):
-            if by_vector:
-                cast(nc.vector.tensor_copy, 0, first, by_vector)
-            if count > by_vector:
-                cast(nc.scalar.copy, 0, first + by_vector, count - by_vector)
         def gpsimd_copy(out, in_):
             nc.gpsimd.tensor_scalar(out=out, in0=in_, scalar1=1.0, scalar2=0.0, op0=MULT, op1=mybir.AluOpType.add)
 
-        for (first, count), by_gpsimd, by_vector in zip(LOADS[1], GPSIMD_CASTS, VECTOR_CASTS[1]):
-            if count > by_gpsimd + by_vector:
-                cast(nc.scalar.copy, 1, first + by_vector, count - by_gpsimd - by_vector)
-            if by_gpsimd:
-                cast(gpsimd_copy, 1, first + count - by_gpsimd, by_gpsimd)
+        for u, first, by_vector, by_scalar, by_gpsimd in CASTS:
+            for copy, count in ((nc.vector.tensor_copy, by_vector), (nc.scalar.copy, by_scalar), (gpsimd_copy, by_gpsimd)):
+                if count:
+                    cast(copy, u, first, count)
+                first += count
 
-        for first in range(0, SLOTS, SPAN):
-            gather(0, first, SPAN)
-        for (first, count), by_vector in zip(LOADS[1], VECTOR_CASTS[1]):
-            if by_vector:
-                cast(nc.vector.tensor_copy, 1, first, by_vector)
+        for i in range(2):
+            nc.vector.tensor_copy(out=early[:, i, :], in_=staged[(0, 0)][:, i, :].indirect(listed(EARLY, SLOTS - EARLY)))
+        gather(0, 0, SPAN)
+        gather(0, SPAN, EARLY - SPAN)
+        nc.scalar.copy(
+            out=picked[EARLY // SPAN][:, 0, EARLY % SPAN :].bitcast(BF16).rearrange("p (d i) -> p d i", i=2),
+            in_=early[:].rearrange("p i d -> p d i"),
+        )
 
         for c in range(CHUNKS):
             gather(1, c * CHUNK, CHUNK)

@@ -23,26 +23,24 @@ CHUNKS = SLOTS // CHUNK
 EXPERTS_PER_CHUNK = CHUNK // C
 EXPERTS_PER_BANK = 2
 
-SPAN = 2048
+SPANS = ((0, 2048), (2048, 1024))
 
 EARLY = 3072
 
-STAGE = (4096, 2048)
+STAGES = (((0, 4096),), ((0, 2048), (2048, 1024), (3072, 1024)))
 LOADS = (
     ((0, 2, 0, 1792), (0, 1, 1792, 2304), (1, 2, 1792, 1024), (1, 2, 2816, 1280)),
-    ((0, 2, 0, 256), (0, 2, 256, 768), (0, 2, 1024, 1024), (0, 2, 2048, 1024), (0, 2, 3072, 512), (0, 2, 3584, 256), (0, 2, 3840, 256)),
+    ((0, 2, 0, 256), (0, 2, 256, 1792), (0, 2, 2048, 1024), (0, 2, 3072, 640), (0, 2, 3712, 384)),
 )
 CASTS = (
     (0, 0, 1152, 640, 0),
     (0, 1792, 0, 576, 448),
     (0, 2816, 0, 704, 576),
     (1, 0, 0, 256, 0),
-    (1, 256, 0, 0, 768),
-    (1, 1024, 0, 576, 448),
+    (1, 256, 0, 960, 832),
     (1, 2048, 0, 576, 448),
-    (1, 3072, 0, 288, 224),
-    (1, 3584, 0, 144, 112),
-    (1, 3840, 0, 144, 112),
+    (1, 3072, 0, 352, 288),
+    (1, 3712, 0, 224, 160),
 )
 
 SCATTERS = ((0, 2048), (2048, 2048))
@@ -58,15 +56,20 @@ def tile_routed_moe_kernel(tc, xT, w_words, w_scales, gate, offs, out):
 
         rows = xT.rearrange("(p t) m -> p t m", t=4)
         staged = {}
+
+        def staged_rows(u, first, count):
+            for s, (start, tokens) in enumerate(STAGES[u]):
+                if start <= first < start + tokens:
+                    return staged[(u, s)][:, :, first - start : first - start + count]
+
         for u in range(2):
-            for s in range(T // STAGE[u]):
+            for s, (start, tokens) in enumerate(STAGES[u]):
                 staged[(u, s)] = sbuf.tile(
-                    [P, 2, STAGE[u]], F32, name="staged%d_%d" % (u, s), tag="bytes%d_%d" % (u, s), align_bytes=64
+                    [P, 2, tokens], F32, name="staged%d_%d" % (u, s), tag="bytes%d_%d" % (u, s), align_bytes=64
                 )
             for row, end, first, count in LOADS[u]:
-                at = first % STAGE[u]
                 nc.sync.dma_start(
-                    staged[(u, first // STAGE[u])][:, row:end, at : at + count],
+                    staged_rows(u, first, count)[:, row:end, :],
                     rows[:, 2 * u + row : 2 * u + end, first : first + count],
                 )
                 if u == 0 and first == 0:
@@ -88,43 +91,47 @@ def tile_routed_moe_kernel(tc, xT, w_words, w_scales, gate, offs, out):
             nc.sync.dma_start(gates[:, first : first + count], gate[:, first : first + count])
 
         window = [sbuf.tile([P, T, 2], BF16, name="window%d" % u) for u in range(2)]
-        picked = [sbuf.tile([P, 2, SPAN], U32, name="picked%d" % h) for h in range(SLOTS // SPAN)]
+        picked = [sbuf.tile([P, 2, count], U32, name="picked%d" % h) for h, (first, count) in enumerate(SPANS)]
+        picked.append(sbuf.tile([P, 2, SLOTS - EARLY], U32, name="picked_early", tag="bytes1_2", align_bytes=64))
         early = sbuf.tile([P, 2, SLOTS - EARLY], F32, name="early")
         grouped = [
-            sbuf.tile([P, 4 * SPAN], BF16, name="grouped%d" % h, tag="bytes1_%d" % h, align_bytes=64)
-            for h in range(SLOTS // SPAN)
+            sbuf.tile([P, 4 * count], BF16, name="grouped%d" % h, tag="bytes1_%d" % h, align_bytes=64)
+            for h, (first, count) in enumerate(SPANS)
         ]
+        grouped.append(sbuf.tile([P, 4 * (SLOTS - EARLY)], BF16, name="grouped_early", align_bytes=64))
         slot_codes = [sbuf.tile([P, CHUNK], U32, name="slot_codes%d" % c, align_bytes=64) for c in range(CHUNKS)]
         slot_scales = [sbuf.tile([P, CHUNK], U8, name="slot_scales%d" % c, align_bytes=64) for c in range(CHUNKS)]
         sums = sbuf.tile([P, SLOTS], F32, name="sums")
         result = sbuf.tile([P, T], F32, name="result")
 
         def cast(copy, u, first, count):
-            at = first % STAGE[u]
-            copy(
-                out=window[u][:, first : first + count, :],
-                in_=staged[(u, first // STAGE[u])][:, :, at : at + count].rearrange("p i m -> p m i"),
-            )
+            copy(out=window[u][:, first : first + count, :], in_=staged_rows(u, first, count).rearrange("p i m -> p m i"))
 
         def listed(first, count):
             return offsets[:, first // PER_COLUMN : (first + count) // PER_COLUMN]
 
+        def place(first):
+            for h, (start, count) in enumerate(SPANS):
+                if start <= first < start + count:
+                    return h, first - start
+            return len(SPANS), first - EARLY
+
         def gather(u, first, count):
-            at = first % SPAN
+            h, at = place(first)
             nc.vector.tensor_copy(
-                out=picked[first // SPAN][:, u, at : at + count],
+                out=picked[h][:, u, at : at + count],
                 in_=window[u][:].rearrange("p m i -> p (m i)").bitcast(U32).indirect(listed(first, count)),
             )
 
         def four_values(c):
-            at = c * CHUNK % SPAN
-            return grouped[c * CHUNK // SPAN][:, 4 * at : 4 * (at + CHUNK)]
+            h, at = place(c * CHUNK)
+            return grouped[h][:, 4 * at : 4 * (at + CHUNK)]
 
         def interleave(c):
-            at = c * CHUNK % SPAN
+            h, at = place(c * CHUNK)
             nc.scalar.copy(
                 out=four_values(c).bitcast(U32).rearrange("p (d u) -> p d u", u=2),
-                in_=picked[c * CHUNK // SPAN][:, :, at : at + CHUNK].rearrange("p u d -> p d u"),
+                in_=picked[h][:, :, at : at + CHUNK].rearrange("p u d -> p d u"),
             )
 
         def quantise(c):
@@ -167,10 +174,10 @@ def tile_routed_moe_kernel(tc, xT, w_words, w_scales, gate, offs, out):
 
         for i in range(2):
             nc.vector.tensor_copy(out=early[:, i, :], in_=staged[(0, 0)][:, i, :].indirect(listed(EARLY, SLOTS - EARLY)))
-        gather(0, 0, SPAN)
-        gather(0, SPAN, EARLY - SPAN)
-        nc.scalar.copy(
-            out=picked[EARLY // SPAN][:, 0, EARLY % SPAN :].bitcast(BF16).rearrange("p (d i) -> p d i", i=2),
+        for first, count in SPANS:
+            gather(0, first, count)
+        gpsimd_copy(
+            out=picked[-1][:, 0, :].bitcast(BF16).rearrange("p (d i) -> p d i", i=2),
             in_=early[:].rearrange("p i d -> p d i"),
         )
 

from contextlib import ExitStack

import concourse.mybir as mybir

K, T, E, C, N = 512, 4096, 16, 256, 128
FLOPS = 2 * K * N * E * C

F32 = mybir.dt.float32
BF16 = mybir.dt.bfloat16
I32 = mybir.dt.int32
U32 = mybir.dt.uint32
U16 = mybir.dt.uint16
U8 = mybir.dt.uint8
FP8X4 = mybir.dt.float8_e4m3fn_x4
MULT = mybir.AluOpType.mult

P = 128
SLOTS = E * C
PER_COLUMN = 16

CHUNK = 1024
CHUNKS = SLOTS // CHUNK
EXPERTS_PER_CHUNK = CHUNK // C
EXPERTS_PER_BANK = 2

SPANS = ((0, 2048), (2048, 1024))

EARLY = 3072

STAGES = (((0, 4096),), ((0, 2048), (2048, 1024), (3072, 1024)))
LOADS = (
    ((0, 2, 0, 1792), (0, 1, 1792, 2304), (1, 2, 1792, 1024), (1, 2, 2816, 1280)),
    ((0, 2, 0, 256), (0, 2, 256, 1792), (0, 2, 2048, 1024), (0, 2, 3072, 640), (0, 2, 3712, 384)),
)
CASTS = (
    (0, 0, 1152, 640, 0),
    (0, 1792, 0, 576, 448),
    (0, 2816, 0, 704, 576),
    (1, 0, 0, 256, 0),
    (1, 256, 0, 960, 832),
    (1, 2048, 0, 576, 448),
    (1, 3072, 0, 352, 288),
    (1, 3712, 0, 224, 160),
)

SCATTERS = ((0, 2048), (2048, 2048))


def tile_routed_moe_kernel(tc, xT, w_words, w_scales, gate, offs, out):
    nc = tc.nc
    with ExitStack() as ctx:
        sbuf = ctx.enter_context(tc.tile_pool(name="sbuf", bufs=1))
        psum = ctx.enter_context(tc.psum_pool(name="psum", bufs=1))

        offsets = sbuf.tile([P, SLOTS // PER_COLUMN], U16, name="offsets")

        rows = xT.rearrange("(p t) m -> p t m", t=4)
        staged = {}

        def staged_rows(u, first, count):
            for s, (start, tokens) in enumerate(STAGES[u]):
                if start <= first < start + tokens:
                    return staged[(u, s)][:, :, first - start : first - start + count]

        for u in range(2):
            for s, (start, tokens) in enumerate(STAGES[u]):
                staged[(u, s)] = sbuf.tile(
                    [P, 2, tokens], F32, name="staged%d_%d" % (u, s), tag="bytes%d_%d" % (u, s), align_bytes=64
                )
            for row, end, first, count in LOADS[u]:
                nc.sync.dma_start(
                    staged_rows(u, first, count)[:, row:end, :],
                    rows[:, 2 * u + row : 2 * u + end, first : first + count],
                )
                if u == 0 and first == 0:
                    nc.sync.dma_start(offsets[:], offs)

        weight_codes = sbuf.tile([P, E, 4 * N], U8, name="weight_codes", align_bytes=64)
        nc.sync.dma_start(
            weight_codes[:].bitcast(I32), w_words.rearrange("e a p n r -> p (e a) (n r)").bitcast(I32)
        )
        weight_scales = sbuf.tile([P, E * N], U8, name="weight_scales", align_bytes=64)
        nc.vector.memset(weight_scales[:].bitcast(I32), 0)
        for quadrant in range(4):
            nc.sync.dma_start(
                weight_scales[32 * quadrant : 32 * quadrant + 4, :].bitcast(I32).rearrange("q (e n) -> q e n", e=E),
                w_scales[:, 0, 4 * quadrant : 4 * quadrant + 4, :].bitcast(I32).rearrange("e q n -> q e n"),
            )
        gates = sbuf.tile([P, SLOTS], F32, name="gates")
        for first, count in SCATTERS:
            nc.sync.dma_start(gates[:, first : first + count], gate[:, first : first + count])

        window = [sbuf.tile([P, T, 2], BF16, name="window%d" % u) for u in range(2)]
        picked = [sbuf.tile([P, 2, count], U32, name="picked%d" % h) for h, (first, count) in enumerate(SPANS)]
        picked.append(sbuf.tile([P, 2, SLOTS - EARLY], U32, name="picked_early", tag="bytes1_2", align_bytes=64))
        early = sbuf.tile([P, 2, SLOTS - EARLY], F32, name="early")
        grouped = [
            sbuf.tile([P, 4 * count], BF16, name="grouped%d" % h, tag="bytes1_%d" % h, align_bytes=64)
            for h, (first, count) in enumerate(SPANS)
        ]
        grouped.append(sbuf.tile([P, 4 * (SLOTS - EARLY)], BF16, name="grouped_early", align_bytes=64))
        slot_codes = [sbuf.tile([P, CHUNK], U32, name="slot_codes%d" % c, align_bytes=64) for c in range(CHUNKS)]
        slot_scales = [sbuf.tile([P, CHUNK], U8, name="slot_scales%d" % c, align_bytes=64) for c in range(CHUNKS)]
        sums = sbuf.tile([P, SLOTS], F32, name="sums")
        result = sbuf.tile([P, T], F32, name="result")

        def cast(copy, u, first, count):
            copy(out=window[u][:, first : first + count, :], in_=staged_rows(u, first, count).rearrange("p i m -> p m i"))

        def listed(first, count):
            return offsets[:, first // PER_COLUMN : (first + count) // PER_COLUMN]

        def place(first):
            for h, (start, count) in enumerate(SPANS):
                if start <= first < start + count:
                    return h, first - start
            return len(SPANS), first - EARLY

        def gather(u, first, count):
            h, at = place(first)
            nc.vector.tensor_copy(
                out=picked[h][:, u, at : at + count],
                in_=window[u][:].rearrange("p m i -> p (m i)").bitcast(U32).indirect(listed(first, count)),
            )

        def four_values(c):
            h, at = place(c * CHUNK)
            return grouped[h][:, 4 * at : 4 * (at + CHUNK)]

        def interleave(c):
            h, at = place(c * CHUNK)
            nc.scalar.copy(
                out=four_values(c).bitcast(U32).rearrange("p (d u) -> p d u", u=2),
                in_=picked[h][:, :, at : at + CHUNK].rearrange("p u d -> p d u"),
            )

        def quantise(c):
            nc.vector.quantize_mx(out=slot_codes[c][:].bitcast(FP8X4), scales=slot_scales[c][:], in_=four_values(c))

        def multiply(c):
            for bank_no in range(EXPERTS_PER_CHUNK // EXPERTS_PER_BANK):
                bank = psum.tile([P, EXPERTS_PER_BANK * C], F32, name="bank%d_%d" % (c, bank_no))
                for side in range(EXPERTS_PER_BANK):
                    at = (bank_no * EXPERTS_PER_BANK + side) * C
                    e = (c * CHUNK + at) // C
                    nc.tensor.matmul_mx(
                        out=bank[:, side * C : (side + 1) * C],
                        lhsT=weight_codes[:, e, :].bitcast(FP8X4),
                        lhsT_scale=weight_scales[:, e * N : (e + 1) * N],
                        rhs=slot_codes[c][:, at : at + C].bitcast(FP8X4),
                        rhs_scale=slot_scales[c][:, at : at + C],
                        start=True,
                        stop=True,
                    )
                first = c * CHUNK + bank_no * EXPERTS_PER_BANK * C
                nc.scalar.copy(out=sums[:, first : first + EXPERTS_PER_BANK * C], in_=bank[:])

        def scatter(first, count):
            nc.vector.tensor_tensor(
                out=result[:].indirect(listed(first, count)),
                in0=sums[:, first : first + count],
                in1=gates[:, first : first + count],
                op=MULT,
            )

        def gpsimd_copy(out, in_):
            nc.gpsimd.tensor_scalar(out=out, in0=in_, scalar1=1.0, scalar2=0.0, op0=MULT, op1=mybir.AluOpType.add)

        for u, first, by_vector, by_scalar, by_gpsimd in CASTS:
            for copy, count in ((nc.vector.tensor_copy, by_vector), (nc.scalar.copy, by_scalar), (gpsimd_copy, by_gpsimd)):
                if count:
                    cast(copy, u, first, count)
                first += count

        for i in range(2):
            nc.vector.tensor_copy(out=early[:, i, :], in_=staged[(0, 0)][:, i, :].indirect(listed(EARLY, SLOTS - EARLY)))
        for first, count in SPANS:
            gather(0, first, count)
        gpsimd_copy(
            out=picked[-1][:, 0, :].bitcast(BF16).rearrange("p (d i) -> p d i", i=2),
            in_=early[:].rearrange("p i d -> p d i"),
        )

        for c in range(CHUNKS):
            gather(1, c * CHUNK, CHUNK)
            interleave(c)
        for c in range(CHUNKS):
            quantise(c)
            multiply(c)
        for first, count in SCATTERS:
            scatter(first, count)

        quarter = T // 4
        for h, queue in enumerate((nc.sync, nc.scalar, nc.sync, nc.scalar)):
            queue.dma_start(out[:, h * quarter : (h + 1) * quarter], result[:, h * quarter : (h + 1) * quarter])
